import numpy as np
import ml_dtypes


def mxq(x, axis, fmt="e4m3"):
    dtype, down = {"e4m3": (ml_dtypes.float8_e4m3fn, 7), "e5m2": (ml_dtypes.float8_e5m2, 14)}[fmt]
    v = np.moveaxis(np.asarray(x, np.float32).astype(ml_dtypes.bfloat16).astype(np.float64), axis, -1)
    blocks = v.reshape(v.shape[:-1] + (-1, 32))
    amax = np.abs(blocks).max(-1, keepdims=True)
    byte = np.maximum(np.where(amax > 0, np.frexp(amax)[1] - 1 + 127, 0) - down, 1)
    scale = np.exp2(byte - 127.0)
    codes = (blocks / scale).astype(np.float32).astype(dtype).astype(np.float64)
    return np.moveaxis((codes * scale).reshape(v.shape), -1, axis)


WIDE = False


def mx_kscale(k):
    if not WIDE:
        return np.ones(k)
    levels = np.array([10, -10, 5, -5, 0])
    if k % 512:
        return np.exp2(np.random.permutation(np.resize(levels, k // 32))).repeat(32)
    a = np.empty((k // 512, 16))
    for p in range(k // 512):
        a[p, :8] = np.random.permutation(np.resize(levels, 8))
        for g in range(8):
            far = levels[np.abs(levels - a[p, g]) >= 10]
            a[p, g + 8] = far[np.random.randint(len(far))]
    return np.exp2(a.ravel()).repeat(32)


def f64(x):
    return np.asarray(x).astype(np.float64)


def striped(idx):
    return np.tile(np.asarray(idx).reshape(-1, 16).T, (8, 1)).astype(np.uint16)


def unstriped(offs):
    return offs[:16].T.reshape(-1).astype(np.int64)


E2M1 = np.array([0.0, 0.5, 1.0, 1.5, 2.0, 3.0, 4.0, 6.0, -0.0, -0.5, -1.0, -1.5, -2.0, -3.0, -4.0, -6.0])


def pack_weight(w, fmt):
    k, n = w.shape
    w = f64(np.asarray(w, np.float32).astype(ml_dtypes.bfloat16)).reshape(k // 32, 32, n)
    amax = np.abs(w).max(1)
    if fmt == "e4m3":
        byte = np.frexp(amax)[1] - 1 + 127 - 7
    else:
        mant, ex = np.frexp(amax / 6.0)
        byte = np.where(mant > 0.5, ex, ex - 1) + 127
    byte = np.clip(np.where(amax > 0, byte, 1), 1, 254)
    scaled = (w * np.exp2(127.0 - byte)[:, None, :]).reshape(k, n).astype(np.float32)
    by_word = np.ascontiguousarray(scaled.reshape(k // 512, 128, 4, n).transpose(0, 1, 3, 2))
    if fmt == "e4m3":
        words = by_word.astype(ml_dtypes.float8_e4m3fn).view(np.uint8)
    else:
        c = by_word.astype(ml_dtypes.float4_e2m1fn).view(np.uint8) & 0xF
        words = (c[..., 0::2] | (c[..., 1::2] << 4)).reshape(k // 512, 128, 2 * n)
    return np.ascontiguousarray(words), np.ascontiguousarray(byte.astype(np.uint8).reshape(k // 512, 16, n))


def unpack_weight(words, scales, fmt):
    g, _, n = scales.shape
    words = np.ascontiguousarray(words).reshape(g, 128, n, -1)
    if fmt == "e4m3":
        vals = words.view(ml_dtypes.float8_e4m3fn).astype(np.float64)
    else:
        nib = np.empty((g, 128, n, 4), np.uint8)
        nib[..., 0::2] = words & 0xF
        nib[..., 1::2] = words >> 4
        vals = E2M1[nib]
    vals = vals * np.repeat(np.exp2(scales.astype(np.float64) - 127.0), 8, axis=1)[..., None]
    return vals.transpose(0, 1, 3, 2).reshape(g * 512, n)


D, E, T, I, Q = 512, 512, 2048, 512, 128


def setup_inputs():
    n = np.random.standard_normal
    idx2 = np.random.permutation(I)[:I]
    idx = np.random.permutation(T)[:I]
    fd = mx_kscale(D)
    fe = mx_kscale(E)
    keysp = pack_weight(n((D, T)) / fd[:, None], "e2m1")
    valsp = pack_weight(n((E, T)) / fe[:, None], "e2m1")
    return {
        "query": (n((D, Q)) * 0.7 / np.sqrt(D) * fd[:, None]).astype(np.float32),
        "keys_words": keysp[0],
        "keys_scales": keysp[1],
        "gout": (n((E, Q)) * 1 / np.sqrt(E) * fe[:, None]).astype(np.float32),
        "vals_words": valsp[0],
        "vals_scales": valsp[1],
        "dquery": (n((D, Q)) * 1.0 / np.sqrt(D) * fd[:, None]).astype(np.float32),
        "base": (0.5 * n((Q, T))).astype(np.float32),
        "offs2": striped(idx2),
        "offs": striped(idx),
    }


def reference(query, keys_words, keys_scales, gout, vals_words, vals_scales, dquery, base, offs2, offs):
    idx2 = unstriped(offs2)
    idx = unstriped(offs)
    keysu = unpack_weight(keys_words, keys_scales, "e2m1")
    valsu = unpack_weight(vals_words, vals_scales, "e2m1")
    queryq = mxq(f64(query), 0, "e4m3")
    keysidxg = keysu[:, idx]
    a = queryq.T @ keysidxg
    dqueryq = mxq(f64(dquery), 0, "e4m3")
    ta = dqueryq.T @ keysidxg
    pa = np.exp(a)
    pb = np.sqrt(pa)
    p = pa * pb[:, idx2]
    z = np.sum(p, axis=1, keepdims=True)
    goutq = mxq(f64(gout), 0, "e4m3")
    valsidxg = valsu[:, idx]
    c0 = goutq.T @ valsidxg
    dz = np.sum(c0 * p / np.square(z) * (-1.0), axis=1, keepdims=True)
    dp = c0 / z + dz
    e1 = dp * pa
    s1 = np.zeros((Q, I))
    s1[:, idx2] = e1
    dpa = dp * pb[:, idx2] + s1 * 0.5 / np.sqrt(pa)
    tpa = ta * pa
    tpb = tpa * 0.5 / pb
    tp = tpa * pb[:, idx2] + tpb[:, idx2] * pa
    tz = np.sum(tp, axis=1, keepdims=True)
    tdz = np.sum((tp * c0 - tz * z * 2.0 * c0 * p / np.square(z)) / np.square(z) * (-1.0), axis=1, keepdims=True)
    tdp = tz * c0 / np.square(z) * (-1.0) + tdz
    te1 = tdp * pa + tpa * dp
    ts1 = np.zeros((Q, I))
    ts1[:, idx2] = te1
    tdpa = tdp * pb[:, idx2] + tpb[:, idx2] * dp + (ts1 * 0.5 - tpa * 0.5 / np.sqrt(pa) * s1 * 0.5 / np.sqrt(pa)) / np.sqrt(pa)
    tda = tdpa * pa + tpa * dpa
    gs = tda * 512.0
    gf = np.zeros((Q, T))
    gf[:, idx] = gs
    y = f64(base) + gf
    return y

@@ -1,0 +1,166 @@
+from contextlib import ExitStack
+
+import concourse.mybir as mybir
+
+F32 = mybir.dt.float32
+BF16 = mybir.dt.bfloat16
+I32 = mybir.dt.int32
+U32 = mybir.dt.uint32
+U16 = mybir.dt.uint16
+U8 = mybir.dt.uint8
+FP8X4 = mybir.dt.float8_e4m3fn_x4
+FP4X4 = mybir.dt.float4_e2m1fn_x4
+ALU = mybir.AluOpType
+ACT = mybir.ActivationFunctionType
+
+P = 128
+PACK = 4
+T = 2048
+I = 512
+Q = 128
+GATHER_WINDOW = I + 16
+SCATTER_WINDOW = 704
+STORE_WIDTHS = (256, 512, 512, 512, 256)
+
+FLOPS = 3 * 2 * Q * 512 * I
+
+
+def tile_attend_hvlinkedproduct_s_kernel(tc, query, keys_words, keys_scales, gout, vals_words, vals_scales,
+                                          dquery, base, offs2, offs, out):
+    nc = tc.nc
+    with ExitStack() as ctx:
+        sb = ctx.enter_context(tc.tile_pool(name="sb", bufs=1))
+        ps = ctx.enter_context(tc.psum_pool(name="ps", bufs=1))
+
+        def tile(name, cols, dtype=F32):
+            return sb.tile([P, cols], dtype, name=name, align_bytes=64)
+
+        tok_list = tile("tok_list", I // 16, U16)
+        link_list = tile("link_list", I // 16, U16)
+        k_bytes = tile("k_bytes", T, U8)
+        v_bytes = tile("v_bytes", T, U8)
+        k_words = tile("k_words", T, U16)
+        v_words = tile("v_words", T, U16)
+        q_raw = tile("q_raw", PACK * Q)
+        dq_raw = tile("dq_raw", PACK * Q)
+        g_raw = tile("g_raw", PACK * Q)
+        base_sb = tile("base_sb", T)
+        placed = tile("placed", T)
+        pb = tile("pb", GATHER_WINDOW)
+        tpb = tile("tpb", GATHER_WINDOW)
+        warm = tile("warm", 16)
+
+        nc.vector.memset(k_bytes[:].bitcast(I32), 0)
+        nc.vector.memset(v_bytes[:].bitcast(I32), 0)
+        nc.vector.memset(pb[:, I:], 0.0)
+        nc.vector.memset(tpb[:, I:], 0.0)
+        nc.vector.memset(placed[:], 0.0)
+        nc.scalar.activation(warm[:], pb[:, I:], ACT.Exp)
+
+        def load_scale_rows(dst, src):
+            for quad in range(4):
+                nc.sync.dma_start(dst[32 * quad:32 * quad + 4, :].bitcast(I32),
+                                  src[0, 4 * quad:4 * quad + 4, :].bitcast(I32))
+
+        def load_rows(dst, src):
+            nc.sync.dma_start(dst[:], src.rearrange("(p j) q -> p (j q)", j=PACK))
+
+        nc.sync.dma_start(tok_list[:], offs)
+        nc.sync.dma_start(k_words[:].bitcast(I32), keys_words[0].bitcast(I32))
+        load_scale_rows(k_bytes, keys_scales)
+        load_rows(q_raw, query)
+        load_rows(dq_raw, dquery)
+        load_scale_rows(v_bytes, vals_scales)
+        nc.sync.dma_start(v_words[:].bitcast(I32), vals_words[0].bitcast(I32))
+        load_rows(g_raw, gout)
+        nc.sync.dma_start(link_list[:], offs2)
+        nc.sync.dma_start(base_sb[:], base)
+
+        def interleave(name, raw):
+            grouped = tile(name + "_bf", PACK * Q, BF16)
+            nc.scalar.copy(grouped[:].rearrange("p (q j) -> p q j", j=PACK),
+                           raw[:].rearrange("p (j q) -> p q j", j=PACK))
+            return grouped
+
+        def quantise(name, grouped):
+            codes = tile(name + "_codes", Q, U32)
+            scales = tile(name + "_scales", Q, U8)
+            nc.vector.quantize_mx(out=codes[:].bitcast(FP8X4), scales=scales[:], in_=grouped[:])
+            return codes, scales
+
+        def gather(name, window, dtype):
+            picked = tile(name, I, dtype)
+            nc.vector.tensor_copy(picked[:], window[:].indirect(tok_list[:]))
+            return picked
+
+        def product(name, rows, words, scale_bytes):
+            acc = ps.tile([Q, I], F32, name=name)
+            nc.tensor.matmul_mx(out=acc[:], lhsT=rows[0][:].bitcast(FP8X4), lhsT_scale=rows[1][:],
+                                rhs=words[:].bitcast(FP4X4), rhs_scale=scale_bytes[:], start=True, stop=True)
+            return acc
+
+        kg_words = gather("kg_words", k_words, U16)
+        kg_bytes = gather("kg_bytes", k_bytes, U8)
+        q_mx = quantise("q", interleave("q", q_raw))
+        a = product("a", q_mx, kg_words, kg_bytes)
+        dq_mx = quantise("dq", interleave("dq", dq_raw))
+        ta = product("ta", dq_mx, kg_words, kg_bytes)
+
+        root4 = tile("root4", I)
+        root4_sum = tile("root4_sum", 1)
+        root4_inv = tile("root4_inv", 1)
+        pa = tile("pa", I)
+        nc.scalar.activation(root4[:], a[:], ACT.Exp, scale=0.25, accum_out=root4_sum[:])
+        vg_bytes = gather("vg_bytes", v_bytes, U8)
+        nc.vector.reciprocal(root4_inv[:], root4_sum[:])
+        nc.scalar.activation(pb[:, :I], root4[:], ACT.Square, scale=root4_inv[:])
+        nc.scalar.activation(pa[:], pb[:, :I], ACT.Square)
+        vg_words = gather("vg_words", v_words, U16)
+        g_grouped = interleave("g", g_raw)
+
+        nc.vector.scalar_tensor_tensor(tpb[:, :I], ta[:], 0.5, pb[:, :I], ALU.mult, ALU.mult)
+        p = tile("p", I)
+        nc.vector.tensor_tensor(p[:], pb[:].indirect(link_list[:]), pa[:], ALU.mult)
+        g_mx = quantise("g", g_grouped)
+        c0 = product("c0", g_mx, vg_words, vg_bytes)
+
+        p_small = tile("p_small", I)
+        z_small = tile("z_small", 1)
+        s = tile("s", 1)
+        w = tile("w", I)
+        nc.scalar.activation(p_small[:], p[:], ACT.Copy, scale=1.0 / 256.0, accum_out=z_small[:])
+        hp = tile("hp", I)
+        pt = tile("pt", I)
+        cs = tile("cs", I)
+        nc.vector.tensor_tensor(pt[:], ta[:], p[:], ALU.mult)
+        nc.vector.tensor_tensor(hp[:], tpb[:].indirect(link_list[:]), pa[:], ALU.mult)
+        nc.vector.reciprocal(s[:], z_small[:])
+        nc.scalar.activation(w[:], p_small[:], ACT.Copy, scale=s[:])
+        nc.scalar.activation(cs[:], c0[:], ACT.Copy, scale=s[:])
+
+        tp = tile("tp", I)
+        tz = tile("tz", 1)
+        cw = tile("cw", I)
+        cbar = tile("cbar", 1)
+        m = tile("m", I)
+        n = tile("n", I)
+        nsum = tile("nsum", 1)
+        half = tile("half", I)
+        nc.vector.scalar_tensor_tensor(tp[:], hp[:], 1.0, pt[:], ALU.mult, ALU.add, accum_out=tz[:])
+        nc.vector.scalar_tensor_tensor(cw[:], c0[:], s[:], w[:], ALU.mult, ALU.mult, accum_out=cbar[:])
+        nc.vector.scalar_tensor_tensor(m[:], w[:], tz[:], tp[:], ALU.mult, ALU.subtract)
+        nc.vector.scalar_tensor_tensor(n[:], cs[:], cbar[:], m[:], ALU.subtract, ALU.mult, accum_out=nsum[:])
+        nc.vector.scalar_tensor_tensor(half[:], w[:], nsum[:], n[:], ALU.mult, ALU.subtract)
+
+        linked = tile("linked", SCATTER_WINDOW)
+        whole = tile("whole", I)
+        nc.vector.tensor_copy(linked[:].indirect(link_list[:]), half[:])
+        nc.scalar.activation(whole[:], half[:], ACT.Copy, scale=2.0)
+        nc.vector.tensor_tensor(placed[:].indirect(tok_list[:]), linked[:, :I], whole[:], ALU.add)
+
+        first = 0
+        for width in STORE_WIDTHS:
+            cols = slice(first, first + width)
+            nc.vector.tensor_tensor(base_sb[:, cols], base_sb[:, cols], placed[:, cols], ALU.add)
+            nc.sync.dma_start(out[:, cols], base_sb[:, cols])
+            first += width

@@ -1,6 +1,7 @@
 from contextlib import ExitStack
 
 import concourse.mybir as mybir
+from concourse.masks import make_identity
 
 F32 = mybir.dt.float32
 BF16 = mybir.dt.bfloat16
@@ -19,7 +20,7 @@ T = 2048
 I = 512
 Q = 128
 GATHER_WINDOW = I + 16
-SCATTER_WINDOW = 704
+SCATTER_WINDOW = 1024
 STORE_WIDTHS = (256, 512, 512, 512, 256)
 
 FLOPS = 3 * 2 * Q * 512 * I
@@ -30,66 +31,66 @@ def tile_attend_hvlinkedproduct_s_kernel(tc, query, keys_words, keys_scales, gou
     nc = tc.nc
     with ExitStack() as ctx:
         sb = ctx.enter_context(tc.tile_pool(name="sb", bufs=1))
+        ov = ctx.enter_context(tc.tile_pool(name="ov", bufs=1))
         ps = ctx.enter_context(tc.psum_pool(name="ps", bufs=1))
 
-        def tile(name, cols, dtype=F32):
-            return sb.tile([P, cols], dtype, name=name, align_bytes=64)
+        def tile(name, cols, dtype=F32, tag=None):
+            return sb.tile([P, cols], dtype, name=name, tag=tag or name, align_bytes=64)
 
         tok_list = tile("tok_list", I // 16, U16)
         link_list = tile("link_list", I // 16, U16)
         k_bytes = tile("k_bytes", T, U8)
-        v_bytes = tile("v_bytes", T, U8)
         k_words = tile("k_words", T, U16)
-        v_words = tile("v_words", T, U16)
-        q_raw = tile("q_raw", PACK * Q)
-        dq_raw = tile("dq_raw", PACK * Q)
-        g_raw = tile("g_raw", PACK * Q)
-        base_sb = tile("base_sb", T)
-        placed = tile("placed", T)
         pb = tile("pb", GATHER_WINDOW)
-        tpb = tile("tpb", GATHER_WINDOW)
-        warm = tile("warm", 16)
+        warm_in = tile("warm_in", 16, tag="warm_then_rows")
+        warm_out = ov.tile([P, 16], F32, name="warm_out", offset=4064)
+        ident = tile("ident", P)
+        make_identity(nc, ident[:])
 
         nc.vector.memset(k_bytes[:].bitcast(I32), 0)
-        nc.vector.memset(v_bytes[:].bitcast(I32), 0)
+        nc.vector.memset(warm_in[:], 0.0)
         nc.vector.memset(pb[:, I:], 0.0)
-        nc.vector.memset(tpb[:, I:], 0.0)
-        nc.vector.memset(placed[:], 0.0)
-        nc.scalar.activation(warm[:], pb[:, I:], ACT.Exp)
+        nc.scalar.activation(warm_out[:], warm_in[:], ACT.Exp)
+        v_bytes = ov.tile([P, T], U8, name="v_bytes", offset=4096)
+        nc.vector.memset(v_bytes[:].bitcast(I32), 0)
 
-        def load_scale_rows(dst, src):
+        def load_scale_rows(queue, dst, src):
             for quad in range(4):
-                nc.sync.dma_start(dst[32 * quad:32 * quad + 4, :].bitcast(I32),
-                                  src[0, 4 * quad:4 * quad + 4, :].bitcast(I32))
+                queue.dma_start(dst[32 * quad:32 * quad + 4, :].bitcast(I32),
+                                src[0, 4 * quad:4 * quad + 4, :].bitcast(I32))
 
         def load_rows(dst, src):
-            nc.sync.dma_start(dst[:], src.rearrange("(p j) q -> p (j q)", j=PACK))
+            nc.sync.dma_start(dst, src.rearrange("(p j) q -> p (j q)", j=PACK))
 
-        nc.sync.dma_start(tok_list[:], offs)
         nc.sync.dma_start(k_words[:].bitcast(I32), keys_words[0].bitcast(I32))
-        load_scale_rows(k_bytes, keys_scales)
+        nc.sync.dma_start(tok_list[:], offs)
+        load_scale_rows(nc.sync, k_bytes, keys_scales)
+        q_tile = tile("q_tile", PACK * Q)
+        q_raw = q_tile[:]
+        rows_raw = tile("rows_raw", 2 * PACK * Q, tag="warm_then_rows")
+        dq_raw, g_raw = (rows_raw[:, j * PACK * Q:(j + 1) * PACK * Q] for j in range(2))
         load_rows(q_raw, query)
-        load_rows(dq_raw, dquery)
-        load_scale_rows(v_bytes, vals_scales)
-        nc.sync.dma_start(v_words[:].bitcast(I32), vals_words[0].bitcast(I32))
-        load_rows(g_raw, gout)
         nc.sync.dma_start(link_list[:], offs2)
-        nc.sync.dma_start(base_sb[:], base)
+        load_rows(dq_raw, dquery)
+        v_words = ov.tile([P, T], U16, name="v_words", offset=0)
+        nc.sync.dma_start(v_words[:].bitcast(I32), vals_words[0].bitcast(I32))
+        load_scale_rows(nc.sync, v_bytes, vals_scales)
+        load_rows(g_raw, gout)
 
-        def interleave(name, raw):
-            grouped = tile(name + "_bf", PACK * Q, BF16)
+        def interleave(name, raw, tag=None):
+            grouped = tile(name + "_bf", PACK * Q, BF16, tag=tag)
             nc.scalar.copy(grouped[:].rearrange("p (q j) -> p q j", j=PACK),
-                           raw[:].rearrange("p (j q) -> p q j", j=PACK))
+                           raw.rearrange("p (j q) -> p q j", j=PACK))
             return grouped
 
-        def quantise(name, grouped):
-            codes = tile(name + "_codes", Q, U32)
+        def quantise(name, grouped, tag=None):
+            codes = tile(name + "_codes", Q, U32, tag=tag)
             scales = tile(name + "_scales", Q, U8)
             nc.vector.quantize_mx(out=codes[:].bitcast(FP8X4), scales=scales[:], in_=grouped[:])
             return codes, scales
 
-        def gather(name, window, dtype):
-            picked = tile(name, I, dtype)
+        def gather(name, window, dtype, tag=None):
+            picked = tile(name, I, dtype, tag=tag)
             nc.vector.tensor_copy(picked[:], window[:].indirect(tok_list[:]))
             return picked
 
@@ -106,56 +107,79 @@ def tile_attend_hvlinkedproduct_s_kernel(tc, query, keys_words, keys_scales, gou
         dq_mx = quantise("dq", interleave("dq", dq_raw))
         ta = product("ta", dq_mx, kg_words, kg_bytes)
 
-        root4 = tile("root4", I)
-        root4_sum = tile("root4_sum", 1)
-        root4_inv = tile("root4_inv", 1)
+        root4 = tile("root4", I, tag="g_then_hp")
+        root4_sum = tile("root4_sum", 1, tag="sum_then_vg_bytes")
         pa = tile("pa", I)
         nc.scalar.activation(root4[:], a[:], ACT.Exp, scale=0.25, accum_out=root4_sum[:])
-        vg_bytes = gather("vg_bytes", v_bytes, U8)
+        vg_words = gather("vg_words", v_words, U16)
+        root4_inv = ov.tile([P, 1], F32, name="root4_inv", offset=0)
         nc.vector.reciprocal(root4_inv[:], root4_sum[:])
         nc.scalar.activation(pb[:, :I], root4[:], ACT.Square, scale=root4_inv[:])
         nc.scalar.activation(pa[:], pb[:, :I], ACT.Square)
-        vg_words = gather("vg_words", v_words, U16)
-        g_grouped = interleave("g", g_raw)
+        vg_bytes = gather("vg_bytes", v_bytes, U8, tag="sum_then_vg_bytes")
+        g_grouped = interleave("g", g_raw, tag="g_then_hp")
+        base_sb = tile("base_sb", T, tag="warm_then_rows")
+        nc.sync.dma_start(base_sb[:], base)
+        tpb = ov.tile([P, GATHER_WINDOW], F32, name="tpb", offset=5120)
+        nc.gpsimd.memset(tpb[:, I:], 0.0)
 
         nc.vector.scalar_tensor_tensor(tpb[:, :I], ta[:], 0.5, pb[:, :I], ALU.mult, ALU.mult)
-        p = tile("p", I)
+        p = ov.tile([P, I], F32, name="p", offset=3072)
         nc.vector.tensor_tensor(p[:], pb[:].indirect(link_list[:]), pa[:], ALU.mult)
-        g_mx = quantise("g", g_grouped)
+        g_mx = quantise("g", g_grouped, tag="g_codes_then_placed")
         c0 = product("c0", g_mx, vg_words, vg_bytes)
+        placed = tile("placed", T, tag="g_codes_then_placed")
+        nc.gpsimd.memset(placed[:], 0.0)
 
         p_small = tile("p_small", I)
         z_small = tile("z_small", 1)
         s = tile("s", 1)
         w = tile("w", I)
         nc.scalar.activation(p_small[:], p[:], ACT.Copy, scale=1.0 / 256.0, accum_out=z_small[:])
-        hp = tile("hp", I)
+        hp = tile("hp", I, tag="g_then_hp")
         pt = tile("pt", I)
-        cs = tile("cs", I)
-        nc.vector.tensor_tensor(pt[:], ta[:], p[:], ALU.mult)
         nc.vector.tensor_tensor(hp[:], tpb[:].indirect(link_list[:]), pa[:], ALU.mult)
         nc.vector.reciprocal(s[:], z_small[:])
         nc.scalar.activation(w[:], p_small[:], ACT.Copy, scale=s[:])
-        nc.scalar.activation(cs[:], c0[:], ACT.Copy, scale=s[:])
 
         tp = tile("tp", I)
         tz = tile("tz", 1)
         cw = tile("cw", I)
         cbar = tile("cbar", 1)
-        m = tile("m", I)
-        n = tile("n", I)
-        nsum = tile("nsum", 1)
-        half = tile("half", I)
-        nc.vector.scalar_tensor_tensor(tp[:], hp[:], 1.0, pt[:], ALU.mult, ALU.add, accum_out=tz[:])
-        nc.vector.scalar_tensor_tensor(cw[:], c0[:], s[:], w[:], ALU.mult, ALU.mult, accum_out=cbar[:])
-        nc.vector.scalar_tensor_tensor(m[:], w[:], tz[:], tp[:], ALU.mult, ALU.subtract)
-        nc.vector.scalar_tensor_tensor(n[:], cs[:], cbar[:], m[:], ALU.subtract, ALU.mult, accum_out=nsum[:])
-        nc.vector.scalar_tensor_tensor(half[:], w[:], nsum[:], n[:], ALU.mult, ALU.subtract)
+        neg_c = tile("neg_c", I)
+        d = tile("d", I)
+        k = tile("k", I)
+        ksum = tile("ksum", 1)
+        y = tile("y", I)
+        nc.vector.scalar_tensor_tensor(pt[:], ta[:], s[:], p[:], ALU.mult, ALU.mult)
+        nc.vector.scalar_tensor_tensor(cw[:], c0[:], s[:], p_small[:], ALU.mult, ALU.mult, accum_out=cbar[:])
+        nc.scalar.activation(neg_c[:], c0[:], ACT.Identity, scale=-1.0, bias=cbar[:])
+        nc.vector.scalar_tensor_tensor(tp[:], hp[:], s[:], pt[:], ALU.mult, ALU.add, accum_out=tz[:])
+        nc.scalar.activation(d[:], neg_c[:], ACT.Copy, scale=tz[:])
+        nc.vector.scalar_tensor_tensor(k[:], c0[:], cbar[:], tp[:], ALU.subtract, ALU.mult, accum_out=ksum[:])
+        nc.vector.scalar_tensor_tensor(y[:], d[:], ksum[:], w[:], ALU.subtract, ALU.mult)
 
         linked = tile("linked", SCATTER_WINDOW)
+        nc.vector.tensor_tensor(linked[:].indirect(link_list[:]), k[:], y[:], ALU.add)
+
         whole = tile("whole", I)
-        nc.vector.tensor_copy(linked[:].indirect(link_list[:]), half[:])
-        nc.scalar.activation(whole[:], half[:], ACT.Copy, scale=2.0)
+        turned = []
+        for part in range(2):
+            bank = ps.tile([P, 2 * P], F32, name="turn%d" % part)
+            for blk in range(2):
+                src = slice((2 * part + blk) * P, (2 * part + blk + 1) * P)
+                dst = slice(blk * P, (blk + 1) * P)
+                nc.tensor.matmul(bank[:, dst], k[:, src], ident[:], start=True, stop=False, is_transpose=True)
+                nc.tensor.matmul(bank[:, dst], y[:, src], ident[:], start=False, stop=True, is_transpose=True)
+            summed = tile("summed%d" % part, 2 * P)
+            nc.scalar.copy(summed[:], bank[:])
+            turned.append(summed)
+        for part in range(2):
+            bank = ps.tile([P, 2 * P], F32, name="back%d" % part)
+            for blk in range(2):
+                dst = slice(blk * P, (blk + 1) * P)
+                nc.tensor.transpose(bank[:, dst], turned[part][:, dst], ident[:])
+            nc.scalar.activation(whole[:, 2 * part * P:2 * (part + 1) * P], bank[:], ACT.Copy, scale=2.0)
         nc.vector.tensor_tensor(placed[:].indirect(tok_list[:]), linked[:, :I], whole[:], ALU.add)
 
         first = 0

@@ -1,3 +1,4 @@
+import math
 from contextlib import ExitStack
 
 import concourse.mybir as mybir
@@ -42,7 +43,7 @@ def tile_attend_hvlinkedproduct_s_kernel(tc, query, keys_words, keys_scales, gou
         k_bytes = tile("k_bytes", T, U8)
         k_words = tile("k_words", T, U16)
         pb = tile("pb", GATHER_WINDOW)
-        warm_in = tile("warm_in", 16, tag="warm_then_rows")
+        warm_in = tile("warm_in", 16, tag="warm_dq_root4")
         warm_out = ov.tile([P, 16], F32, name="warm_out", offset=4064)
         ident = tile("ident", P)
         make_identity(nc, ident[:])
@@ -60,27 +61,24 @@ def tile_attend_hvlinkedproduct_s_kernel(tc, query, keys_words, keys_scales, gou
                                 src[0, 4 * quad:4 * quad + 4, :].bitcast(I32))
 
         def load_rows(dst, src):
-            nc.sync.dma_start(dst, src.rearrange("(p j) q -> p (j q)", j=PACK))
+            nc.sync.dma_start(dst[:], src.rearrange("(p j) q -> p (j q)", j=PACK))
 
-        nc.sync.dma_start(k_words[:].bitcast(I32), keys_words[0].bitcast(I32))
         nc.sync.dma_start(tok_list[:], offs)
-        load_scale_rows(nc.sync, k_bytes, keys_scales)
-        q_tile = tile("q_tile", PACK * Q)
-        q_raw = q_tile[:]
-        rows_raw = tile("rows_raw", 2 * PACK * Q, tag="warm_then_rows")
-        dq_raw, g_raw = (rows_raw[:, j * PACK * Q:(j + 1) * PACK * Q] for j in range(2))
-        load_rows(q_raw, query)
         nc.sync.dma_start(link_list[:], offs2)
+        nc.sync.dma_start(k_words[:].bitcast(I32), keys_words[0].bitcast(I32))
+        load_scale_rows(nc.sync, k_bytes, keys_scales)
+        q_raw = tile("q_raw", PACK * Q, tag="q_g_base")
+        load_rows(q_raw, query)
+        dq_raw = tile("dq_raw", PACK * Q, tag="warm_dq_root4")
         load_rows(dq_raw, dquery)
         v_words = ov.tile([P, T], U16, name="v_words", offset=0)
         nc.sync.dma_start(v_words[:].bitcast(I32), vals_words[0].bitcast(I32))
         load_scale_rows(nc.sync, v_bytes, vals_scales)
-        load_rows(g_raw, gout)
 
         def interleave(name, raw, tag=None):
             grouped = tile(name + "_bf", PACK * Q, BF16, tag=tag)
             nc.scalar.copy(grouped[:].rearrange("p (q j) -> p q j", j=PACK),
-                           raw.rearrange("p (j q) -> p q j", j=PACK))
+                           raw[:].rearrange("p (j q) -> p q j", j=PACK))
             return grouped
 
         def quantise(name, grouped, tag=None):
@@ -104,27 +102,30 @@ def tile_attend_hvlinkedproduct_s_kernel(tc, query, keys_words, keys_scales, gou
         kg_bytes = gather("kg_bytes", k_bytes, U8)
         q_mx = quantise("q", interleave("q", q_raw))
         a = product("a", q_mx, kg_words, kg_bytes)
+        g_raw = tile("g_raw", PACK * Q, tag="q_g_base")
+        load_rows(g_raw, gout)
         dq_mx = quantise("dq", interleave("dq", dq_raw))
         ta = product("ta", dq_mx, kg_words, kg_bytes)
 
-        root4 = tile("root4", I, tag="g_then_hp")
-        root4_sum = tile("root4_sum", 1, tag="sum_then_vg_bytes")
+        root4 = tile("root4", I, tag="warm_dq_root4")
+        root4_sum = tile("root4_sum", 1)
         pa = tile("pa", I)
         nc.scalar.activation(root4[:], a[:], ACT.Exp, scale=0.25, accum_out=root4_sum[:])
         vg_words = gather("vg_words", v_words, U16)
-        root4_inv = ov.tile([P, 1], F32, name="root4_inv", offset=0)
-        nc.vector.reciprocal(root4_inv[:], root4_sum[:])
-        nc.scalar.activation(pb[:, :I], root4[:], ACT.Square, scale=root4_inv[:])
+        shift = tile("shift", 1, tag="g_then_hp")
+        nc.scalar.activation(shift[:], root4_sum[:].bitcast(U32), ACT.Copy,
+                             scale=-2.0 * math.log(2.0) / 2.0 ** 23, bias=2.0 * 127.0 * math.log(2.0))
+        nc.scalar.activation(pb[:, :I], a[:], ACT.Exp, scale=0.5, bias=shift[:])
         nc.scalar.activation(pa[:], pb[:, :I], ACT.Square)
-        vg_bytes = gather("vg_bytes", v_bytes, U8, tag="sum_then_vg_bytes")
+        vg_bytes = gather("vg_bytes", v_bytes, U8)
         g_grouped = interleave("g", g_raw, tag="g_then_hp")
-        base_sb = tile("base_sb", T, tag="warm_then_rows")
+        base_sb = tile("base_sb", T, tag="q_g_base")
         nc.sync.dma_start(base_sb[:], base)
-        tpb = ov.tile([P, GATHER_WINDOW], F32, name="tpb", offset=5120)
+        tpb = ov.tile([P, GATHER_WINDOW], F32, name="tpb", offset=2496)
         nc.gpsimd.memset(tpb[:, I:], 0.0)
 
         nc.vector.scalar_tensor_tensor(tpb[:, :I], ta[:], 0.5, pb[:, :I], ALU.mult, ALU.mult)
-        p = ov.tile([P, I], F32, name="p", offset=3072)
+        p = ov.tile([P, I], F32, name="p", offset=4608)
         nc.vector.tensor_tensor(p[:], pb[:].indirect(link_list[:]), pa[:], ALU.mult)
         g_mx = quantise("g", g_grouped, tag="g_codes_then_placed")
         c0 = product("c0", g_mx, vg_words, vg_bytes)
@@ -136,12 +137,12 @@ def tile_attend_hvlinkedproduct_s_kernel(tc, query, keys_words, keys_scales, gou
         s = tile("s", 1)
         w = tile("w", I)
         nc.scalar.activation(p_small[:], p[:], ACT.Copy, scale=1.0 / 256.0, accum_out=z_small[:])
-        hp = tile("hp", I, tag="g_then_hp")
-        pt = tile("pt", I)
+        hp = tile("hp", I)
         nc.vector.tensor_tensor(hp[:], tpb[:].indirect(link_list[:]), pa[:], ALU.mult)
         nc.vector.reciprocal(s[:], z_small[:])
         nc.scalar.activation(w[:], p_small[:], ACT.Copy, scale=s[:])
 
+        pt = tile("pt", I, tag="g_then_hp")
         tp = tile("tp", I)
         tz = tile("tz", 1)
         cw = tile("cw", I)

import math
from contextlib import ExitStack

import concourse.mybir as mybir
from concourse.masks import make_identity

F32 = mybir.dt.float32
BF16 = mybir.dt.bfloat16
I32 = mybir.dt.int32
U32 = mybir.dt.uint32
U16 = mybir.dt.uint16
U8 = mybir.dt.uint8
FP8X4 = mybir.dt.float8_e4m3fn_x4
FP4X4 = mybir.dt.float4_e2m1fn_x4
ALU = mybir.AluOpType
ACT = mybir.ActivationFunctionType

P = 128
PACK = 4
T = 2048
I = 512
Q = 128
GATHER_WINDOW = I + 16
SCATTER_WINDOW = 1024
STORE_WIDTHS = (256, 512, 512, 512, 256)

FLOPS = 3 * 2 * Q * 512 * I


def tile_attend_hvlinkedproduct_s_kernel(tc, query, keys_words, keys_scales, gout, vals_words, vals_scales,
                                          dquery, base, offs2, offs, out):
    nc = tc.nc
    with ExitStack() as ctx:
        sb = ctx.enter_context(tc.tile_pool(name="sb", bufs=1))
        ov = ctx.enter_context(tc.tile_pool(name="ov", bufs=1))
        ps = ctx.enter_context(tc.psum_pool(name="ps", bufs=1))

        def tile(name, cols, dtype=F32, tag=None):
            return sb.tile([P, cols], dtype, name=name, tag=tag or name, align_bytes=64)

        tok_list = tile("tok_list", I // 16, U16)
        link_list = tile("link_list", I // 16, U16)
        k_bytes = tile("k_bytes", T, U8)
        k_words = tile("k_words", T, U16)
        pb = tile("pb", GATHER_WINDOW)
        warm_in = tile("warm_in", 16, tag="warm_dq_root4")
        warm_out = ov.tile([P, 16], F32, name="warm_out", offset=4064)
        ident = tile("ident", P)
        make_identity(nc, ident[:])

        nc.vector.memset(k_bytes[:].bitcast(I32), 0)
        nc.vector.memset(warm_in[:], 0.0)
        nc.vector.memset(pb[:, I:], 0.0)
        nc.scalar.activation(warm_out[:], warm_in[:], ACT.Exp)
        v_bytes = ov.tile([P, T], U8, name="v_bytes", offset=4096)
        nc.vector.memset(v_bytes[:].bitcast(I32), 0)

        def load_scale_rows(queue, dst, src):
            for quad in range(4):
                queue.dma_start(dst[32 * quad:32 * quad + 4, :].bitcast(I32),
                                src[0, 4 * quad:4 * quad + 4, :].bitcast(I32))

        def load_rows(dst, src):
            nc.sync.dma_start(dst[:], src.rearrange("(p j) q -> p (j q)", j=PACK))

        nc.sync.dma_start(tok_list[:], offs)
        nc.sync.dma_start(link_list[:], offs2)
        nc.sync.dma_start(k_words[:].bitcast(I32), keys_words[0].bitcast(I32))
        load_scale_rows(nc.sync, k_bytes, keys_scales)
        q_raw = tile("q_raw", PACK * Q, tag="q_g_base")
        load_rows(q_raw, query)
        dq_raw = tile("dq_raw", PACK * Q, tag="warm_dq_root4")
        load_rows(dq_raw, dquery)
        v_words = ov.tile([P, T], U16, name="v_words", offset=0)
        nc.sync.dma_start(v_words[:].bitcast(I32), vals_words[0].bitcast(I32))
        load_scale_rows(nc.sync, v_bytes, vals_scales)

        def interleave(name, raw, tag=None):
            grouped = tile(name + "_bf", PACK * Q, BF16, tag=tag)
            nc.scalar.copy(grouped[:].rearrange("p (q j) -> p q j", j=PACK),
                           raw[:].rearrange("p (j q) -> p q j", j=PACK))
            return grouped

        def quantise(name, grouped, tag=None):
            codes = tile(name + "_codes", Q, U32, tag=tag)
            scales = tile(name + "_scales", Q, U8)
            nc.vector.quantize_mx(out=codes[:].bitcast(FP8X4), scales=scales[:], in_=grouped[:])
            return codes, scales

        def gather(name, window, dtype, tag=None):
            picked = tile(name, I, dtype, tag=tag)
            nc.vector.tensor_copy(picked[:], window[:].indirect(tok_list[:]))
            return picked

        def product(name, rows, words, scale_bytes):
            acc = ps.tile([Q, I], F32, name=name)
            nc.tensor.matmul_mx(out=acc[:], lhsT=rows[0][:].bitcast(FP8X4), lhsT_scale=rows[1][:],
                                rhs=words[:].bitcast(FP4X4), rhs_scale=scale_bytes[:], start=True, stop=True)
            return acc

        kg_words = gather("kg_words", k_words, U16)
        kg_bytes = gather("kg_bytes", k_bytes, U8)
        q_mx = quantise("q", interleave("q", q_raw))
        a = product("a", q_mx, kg_words, kg_bytes)
        g_raw = tile("g_raw", PACK * Q, tag="q_g_base")
        load_rows(g_raw, gout)
        dq_mx = quantise("dq", interleave("dq", dq_raw))
        ta = product("ta", dq_mx, kg_words, kg_bytes)

        root4 = tile("root4", I, tag="warm_dq_root4")
        root4_sum = tile("root4_sum", 1)
        pa = tile("pa", I)
        nc.scalar.activation(root4[:], a[:], ACT.Exp, scale=0.25, accum_out=root4_sum[:])
        vg_words = gather("vg_words", v_words, U16)
        shift = tile("shift", 1, tag="g_then_hp")
        nc.scalar.activation(shift[:], root4_sum[:].bitcast(U32), ACT.Copy,
                             scale=-2.0 * math.log(2.0) / 2.0 ** 23, bias=2.0 * 127.0 * math.log(2.0))
        nc.scalar.activation(pb[:, :I], a[:], ACT.Exp, scale=0.5, bias=shift[:])
        nc.scalar.activation(pa[:], pb[:, :I], ACT.Square)
        vg_bytes = gather("vg_bytes", v_bytes, U8)
        g_grouped = interleave("g", g_raw, tag="g_then_hp")
        base_sb = tile("base_sb", T, tag="q_g_base")
        nc.sync.dma_start(base_sb[:], base)
        tpb = ov.tile([P, GATHER_WINDOW], F32, name="tpb", offset=2496)
        nc.gpsimd.memset(tpb[:, I:], 0.0)

        nc.vector.scalar_tensor_tensor(tpb[:, :I], ta[:], 0.5, pb[:, :I], ALU.mult, ALU.mult)
        p = ov.tile([P, I], F32, name="p", offset=4608)
        nc.vector.tensor_tensor(p[:], pb[:].indirect(link_list[:]), pa[:], ALU.mult)
        g_mx = quantise("g", g_grouped, tag="g_codes_then_placed")
        c0 = product("c0", g_mx, vg_words, vg_bytes)
        placed = tile("placed", T, tag="g_codes_then_placed")
        nc.gpsimd.memset(placed[:], 0.0)

        p_small = tile("p_small", I)
        z_small = tile("z_small", 1)
        s = tile("s", 1)
        w = tile("w", I)
        nc.scalar.activation(p_small[:], p[:], ACT.Copy, scale=1.0 / 256.0, accum_out=z_small[:])
        hp = tile("hp", I)
        nc.vector.tensor_tensor(hp[:], tpb[:].indirect(link_list[:]), pa[:], ALU.mult)
        nc.vector.reciprocal(s[:], z_small[:])
        nc.scalar.activation(w[:], p_small[:], ACT.Copy, scale=s[:])

        pt = tile("pt", I, tag="g_then_hp")
        tp = tile("tp", I)
        tz = tile("tz", 1)
        cw = tile("cw", I)
        cbar = tile("cbar", 1)
        neg_c = tile("neg_c", I)
        d = tile("d", I)
        k = tile("k", I)
        ksum = tile("ksum", 1)
        y = tile("y", I)
        nc.vector.scalar_tensor_tensor(pt[:], ta[:], s[:], p[:], ALU.mult, ALU.mult)
        nc.vector.scalar_tensor_tensor(cw[:], c0[:], s[:], p_small[:], ALU.mult, ALU.mult, accum_out=cbar[:])
        nc.scalar.activation(neg_c[:], c0[:], ACT.Identity, scale=-1.0, bias=cbar[:])
        nc.vector.scalar_tensor_tensor(tp[:], hp[:], s[:], pt[:], ALU.mult, ALU.add, accum_out=tz[:])
        nc.scalar.activation(d[:], neg_c[:], ACT.Copy, scale=tz[:])
        nc.vector.scalar_tensor_tensor(k[:], c0[:], cbar[:], tp[:], ALU.subtract, ALU.mult, accum_out=ksum[:])
        nc.vector.scalar_tensor_tensor(y[:], d[:], ksum[:], w[:], ALU.subtract, ALU.mult)

        linked = tile("linked", SCATTER_WINDOW)
        nc.vector.tensor_tensor(linked[:].indirect(link_list[:]), k[:], y[:], ALU.add)

        whole = tile("whole", I)
        turned = []
        for part in range(2):
            bank = ps.tile([P, 2 * P], F32, name="turn%d" % part)
            for blk in range(2):
                src = slice((2 * part + blk) * P, (2 * part + blk + 1) * P)
                dst = slice(blk * P, (blk + 1) * P)
                nc.tensor.matmul(bank[:, dst], k[:, src], ident[:], start=True, stop=False, is_transpose=True)
                nc.tensor.matmul(bank[:, dst], y[:, src], ident[:], start=False, stop=True, is_transpose=True)
            summed = tile("summed%d" % part, 2 * P)
            nc.scalar.copy(summed[:], bank[:])
            turned.append(summed)
        for part in range(2):
            bank = ps.tile([P, 2 * P], F32, name="back%d" % part)
            for blk in range(2):
                dst = slice(blk * P, (blk + 1) * P)
                nc.tensor.transpose(bank[:, dst], turned[part][:, dst], ident[:])
            nc.scalar.activation(whole[:, 2 * part * P:2 * (part + 1) * P], bank[:], ACT.Copy, scale=2.0)
        nc.vector.tensor_tensor(placed[:].indirect(tok_list[:]), linked[:, :I], whole[:], ALU.add)

        first = 0
        for width in STORE_WIDTHS:
            cols = slice(first, first + width)
            nc.vector.tensor_tensor(base_sb[:, cols], base_sb[:, cols], placed[:, cols], ALU.add)
            nc.sync.dma_start(out[:, cols], base_sb[:, cols])
            first += width
